import numpy as np
import ml_dtypes


def mxq(x, axis, fmt="e4m3"):
    dtype, down = {"e4m3": (ml_dtypes.float8_e4m3fn, 7), "e5m2": (ml_dtypes.float8_e5m2, 14)}[fmt]
    v = np.moveaxis(np.asarray(x, np.float32).astype(ml_dtypes.bfloat16).astype(np.float64), axis, -1)
    blocks = v.reshape(v.shape[:-1] + (-1, 32))
    amax = np.abs(blocks).max(-1, keepdims=True)
    byte = np.maximum(np.where(amax > 0, np.frexp(amax)[1] - 1 + 127, 0) - down, 1)
    scale = np.exp2(byte - 127.0)
    codes = (blocks / scale).astype(np.float32).astype(dtype).astype(np.float64)
    return np.moveaxis((codes * scale).reshape(v.shape), -1, axis)


WIDE = False


def mx_kscale(k):
    if not WIDE:
        return np.ones(k)
    levels = np.array([30, -30])
    if k % 512:
        return np.exp2(np.random.permutation(np.resize(levels, k // 32))).repeat(32)
    a = np.empty((k // 512, 16))
    for p in range(k // 512):
        a[p, :8] = np.random.permutation(np.resize(levels, 8))
        for g in range(8):
            far = levels[np.abs(levels - a[p, g]) >= 10]
            a[p, g + 8] = far[np.random.randint(len(far))]
    return np.exp2(a.ravel()).repeat(32)


def f64(x):
    return np.asarray(x).astype(np.float64)


def striped(idx):
    return np.tile(np.asarray(idx).reshape(-1, 16).T, (8, 1)).astype(np.uint16)


def unstriped(offs):
    return offs[:16].T.reshape(-1).astype(np.int64)


def striped8(idx):
    return np.asarray(idx).reshape(8, -1, 16).transpose(0, 2, 1).reshape(128, -1).astype(np.uint16)


def unstriped8(offs):
    return offs.reshape(8, 16, -1).transpose(0, 2, 1).reshape(8, -1).astype(np.int64)


def pick8(x, idx, run):
    r = np.arange(len(x))
    return x[r[:, None], idx[r % (8 * run) // run]]


E2M1 = np.array([0.0, 0.5, 1.0, 1.5, 2.0, 3.0, 4.0, 6.0, -0.0, -0.5, -1.0, -1.5, -2.0, -3.0, -4.0, -6.0])


def pack_weight(w, fmt):
    k, n = w.shape
    w = f64(np.asarray(w, np.float32).astype(ml_dtypes.bfloat16)).reshape(k // 32, 32, n)
    amax = np.abs(w).max(1)
    if fmt in ("e4m3", "e5m2"):
        byte = np.frexp(amax)[1] - 1 + 127 - (7 if fmt == "e4m3" else 14)
    else:
        mant, ex = np.frexp(amax / 6.0)
        byte = np.where(mant > 0.5, ex, ex - 1) + 127
    byte = np.clip(np.where(amax > 0, byte, 1), 1, 254)
    scaled = (w * np.exp2(127.0 - byte)[:, None, :]).reshape(k, n).astype(np.float32)
    by_word = np.ascontiguousarray(scaled.reshape(k // 512, 128, 4, n).transpose(0, 1, 3, 2))
    if fmt in ("e4m3", "e5m2"):
        words = by_word.astype(ml_dtypes.float8_e4m3fn if fmt == "e4m3" else ml_dtypes.float8_e5m2).view(np.uint8)
    else:
        c = by_word.astype(ml_dtypes.float4_e2m1fn).view(np.uint8) & 0xF
        words = (c[..., 0::2] | (c[..., 1::2] << 4)).reshape(k // 512, 128, 2 * n)
    return np.ascontiguousarray(words), np.ascontiguousarray(byte.astype(np.uint8).reshape(k // 512, 16, n))


def unpack_weight(words, scales, fmt):
    g, _, n = scales.shape
    words = np.ascontiguousarray(words).reshape(g, 128, n, -1)
    if fmt in ("e4m3", "e5m2"):
        vals = words.view(ml_dtypes.float8_e4m3fn if fmt == "e4m3" else ml_dtypes.float8_e5m2).astype(np.float64)
    else:
        nib = np.empty((g, 128, n, 4), np.uint8)
        nib[..., 0::2] = words & 0xF
        nib[..., 1::2] = words >> 4
        vals = E2M1[nib]
    vals = vals * np.repeat(np.exp2(scales.astype(np.float64) - 127.0), 8, axis=1)[..., None]
    return vals.transpose(0, 1, 3, 2).reshape(g * 512, n)


K, T, J, R, F, Z, O, U, D, N, S, E = 512, 1024, 256, 512, 512, 1024, 128, 128, 256, 256, 1024, 512


def setup_inputs():
    n = np.random.standard_normal
    idx = np.random.permutation(T)[:J]
    idx2 = np.random.permutation(Z)[:J]
    idx3 = np.stack([np.random.permutation(J)[:O] for _ in range(8)])
    idx4 = np.stack([np.random.permutation(J)[:U] for _ in range(8)])
    idx5 = np.random.permutation(S)[:N]
    idx6 = np.random.permutation(E)[:D]
    idx7 = np.random.permutation(E)[:D]
    ff = mx_kscale(F)
    fk = mx_kscale(K)
    fr = mx_kscale(R)
    xop = pack_weight(n((F, Z)) / ff[:, None], "e5m2")
    wp = pack_weight(n((K, R)) * 1 / np.sqrt(K) / fk[:, None] * fr, "e5m2")
    w2p = pack_weight(n((F, R)) * 1 / np.sqrt(F) * ff[:, None], "e4m3")
    vsp = pack_weight(n((R, S)) * 1 / np.sqrt(R) / fr[:, None], "e4m3")
    return {
        "xo_words": xop[0],
        "xo_scales": xop[1],
        "cq": (np.random.randint(-7, 8, (K, T)).astype(np.float64)).astype(np.float32),
        "gs": (np.random.uniform(0.1, 0.4, (K, 1)) * fk[:, None]).astype(np.float32),
        "w_words": wp[0],
        "w_scales": wp[1],
        "w2_words": w2p[0],
        "w2_scales": w2p[1],
        "vs_words": vsp[0],
        "vs_scales": vsp[1],
        "offs": striped(idx),
        "offs2": striped(idx2),
        "offs3": striped8(idx3),
        "offs4": striped8(idx4),
        "offs5": striped(idx5),
        "offs6": striped(idx6),
        "offs7": striped(idx7),
    }


def reference(xo_words, xo_scales, cq, gs, w_words, w_scales, w2_words, w2_scales, vs_words, vs_scales, offs, offs2, offs3, offs4, offs5, offs6, offs7):
    idx = unstriped(offs)
    idx2 = unstriped(offs2)
    idx3 = unstriped8(offs3)
    idx4 = unstriped8(offs4)
    idx5 = unstriped(offs5)
    idx6 = unstriped(offs6)
    idx7 = unstriped(offs7)
    xou = unpack_weight(xo_words, xo_scales, "e5m2")
    wu = unpack_weight(w_words, w_scales, "e5m2")
    w2u = unpack_weight(w2_words, w2_scales, "e4m3")
    vsu = unpack_weight(vs_words, vs_scales, "e4m3")
    x1 = f64(cq)[:, idx] * f64(gs)
    x1q = mxq(x1, 0, "e4m3")
    a = wu.T @ x1q
    xoidx2g = xou[:, idx2]
    b = w2u.T @ xoidx2g
    lb = b[:, 0:1]
    la = a[:, 0:1]
    h1 = pick8(a, idx3, 64) * lb
    h2 = pick8(b, idx4, 64) * la
    hid = np.concatenate([h1, h2], axis=1)
    vsidx5g = vsu[:, idx5]
    hidq = mxq(hid, 0, "e5m2")
    p = vsidx5g.T @ hidq
    pa = np.zeros((N, E))
    pa[:, idx6] = p
    pb = np.zeros((N, E))
    pb[:, idx7] = p
    y = pa + pb
    return y

@@ -1,0 +1,230 @@
+from contextlib import ExitStack
+
+import concourse.mybir as mybir
+
+F32 = mybir.dt.float32
+BF16 = mybir.dt.bfloat16
+I32 = mybir.dt.int32
+U32 = mybir.dt.uint32
+U16 = mybir.dt.uint16
+U8 = mybir.dt.uint8
+E4M3 = mybir.dt.float8_e4m3fn_x4
+E5M2 = mybir.dt.float8_e5m2_x4
+COPY = mybir.ActivationFunctionType.Copy
+ADD = mybir.AluOpType.add
+
+P = 128
+PACK = 4
+SLOTS = 256
+HALF = 128
+HIDDEN = 512
+TABLE = 1024
+PAGE = 512
+FLOPS = 335544320
+
+
+def tile_list_groupside_codednote_store_pagetwice_kernel(
+    tc, xo_words, xo_scales, cq, gs, w_words, w_scales, w2_words, w2_scales, vs_words, vs_scales,
+    offs, offs2, offs3, offs4, offs5, offs6, offs7, out,
+):
+    nc = tc.nc
+
+    def word_rows(words):
+        return words[0].rearrange("p c i -> p (c i)").bitcast(I32)
+
+    def scale_rows(scales):
+        return scales[0].bitcast(I32).rearrange("(q r) c -> r q c", r=PACK)
+
+    with ExitStack() as ctx:
+        keep = ctx.enter_context(tc.tile_pool(name="keep", bufs=1))
+        psum = ctx.enter_context(tc.psum_pool(name="psum", bufs=1))
+
+        def sb(name, shape, dtype):
+            return keep.tile(shape, dtype, name=name, align_bytes=64)
+
+        def load_list(name, src):
+            tile = sb(name, list(src.shape), U16)
+            nc.sync.dma_start(tile[:], src)
+            return tile
+
+        xo_plane = sb("xo_plane", [P, TABLE], U8)
+        ws_plane = sb("ws_plane", [P, 2 * HIDDEN], U8)
+        vs_plane = sb("vs_plane", [P, TABLE], U8)
+        for plane in (xo_plane, ws_plane, vs_plane):
+            nc.vector.memset(plane[:].bitcast(I32), 0)
+        pages = {}
+        for n in range(2):
+            for which in "ab":
+                pages[which, n] = sb(f"page_{which}{n}", [P, PAGE], F32)
+                nc.vector.memset(pages[which, n][:], 0.0)
+
+        def load_split_scales(name, scales):
+            stage = sb(name, [P, 2, TABLE // 4], I32)
+            for h in range(2):
+                nc.sync.dma_start(stage[64 * h : 64 * h + 4], scale_rows(scales)[:, 2 * h : 2 * h + 2, :])
+            return stage
+
+        def spread_split_scales(plane, stage):
+            for q in range(4):
+                start = 64 * (q // 2)
+                nc.vector.tensor_copy(plane[32 * q : 32 * q + 4, :].bitcast(I32), stage[start : start + 4, q % 2, :])
+
+        xo_raw = sb("xo_raw", [P, TABLE], U32)
+        nc.sync.dma_start(xo_raw[:].bitcast(I32), word_rows(xo_words))
+        slots_xo = load_list("slots_xo", offs2)
+        xo_stage = load_split_scales("xo_stage", xo_scales)
+        ws_stage = sb("ws_stage", [PACK, PACK, 2, HIDDEN // 4], I32)
+        nc.sync.dma_start(ws_stage[:, :, 0, :], scale_rows(w2_scales))
+        nc.sync.dma_start(ws_stage[:, :, 1, :], scale_rows(w_scales))
+        w2_raw = sb("w2_raw", [P, HIDDEN], I32)
+        nc.sync.dma_start(w2_raw[:], word_rows(w2_words))
+        cq_rows = cq.rearrange("(p i) t -> i p t", i=PACK)
+        cq_sb = [sb(f"cq{i}", [P, TABLE], F32) for i in range(PACK)]
+        nc.sync.dma_start(cq_sb[0][:], cq_rows[0])
+        slots_cq = load_list("slots_cq", offs)
+        gs_sb = sb("gs_sb", [P, PACK], F32)
+        nc.sync.dma_start(gs_sb[:], gs.rearrange("(p i) o -> p (i o)", i=PACK))
+        nc.sync.dma_start(cq_sb[1][:], cq_rows[1])
+        vs_stage = load_split_scales("vs_stage", vs_scales)
+        slots_vs = load_list("slots_vs", offs5)
+        for i in range(2, PACK):
+            nc.sync.dma_start(cq_sb[i][:], cq_rows[i])
+        w_raw = sb("w_raw", [P, HIDDEN], I32)
+        nc.sync.dma_start(w_raw[:], word_rows(w_words))
+        late_lists = load_list("late_lists", offs4)
+        vs_raw = sb("vs_raw", [P, TABLE], U32)
+        nc.sync.dma_start(vs_raw[:].bitcast(I32), word_rows(vs_words))
+        place_lists = load_list("place_lists", offs3)
+        cols_a = load_list("cols_a", offs6)
+        cols_b = load_list("cols_b", offs7)
+
+        def deal_words(name, raw, copy, dtype):
+            dealt = sb(name, [P, HIDDEN], U32)
+            copy(
+                dealt[:].bitcast(dtype).rearrange("p (i g m) -> p g i m", i=PACK, m=4),
+                raw[:].bitcast(dtype).rearrange("p (g m i) -> p g i m", i=PACK, m=4),
+            )
+            return dealt
+
+        def weave(name, planes):
+            woven = sb(f"{name}_woven", [P, HALF * PACK], BF16)
+            nc.vector.tensor_copy(
+                woven[:].rearrange("p (g c i) -> p g i c", i=PACK, c=4),
+                planes.rearrange("p i (g c) -> p g i c", c=4),
+            )
+            return woven
+
+        def quantize(name, woven, fmt):
+            codes = sb(f"{name}_codes", [P, HALF], U32)
+            scales = sb(f"{name}_scales", [P, HALF], U8)
+            nc.vector.quantize_mx(out=codes[:].bitcast(fmt), scales=scales[:], in_=woven[:])
+            return codes, scales
+
+        xo_codes = sb("xo_codes", [P, SLOTS], U32)
+        nc.vector.tensor_copy(xo_codes[:], xo_raw[:].indirect(slots_xo[:]))
+        spread_split_scales(xo_plane, xo_stage)
+        xo_sc = sb("xo_sc", [P, SLOTS], U8)
+        nc.vector.tensor_copy(xo_sc[:], xo_plane[:].indirect(slots_xo[:]))
+        for q in range(4):
+            nc.vector.tensor_copy(
+                ws_plane[32 * q : 32 * q + 4, :].bitcast(I32), ws_stage[:, q].rearrange("p s c -> p (s c)")
+            )
+        ws_dealt = sb("ws_dealt", [P, 2, PACK, P], U8)
+        nc.vector.tensor_copy(
+            ws_dealt[:].rearrange("p s i (g m) -> p s g i m", m=16),
+            ws_plane[:].rearrange("p (s g m i) -> p s g i m", s=2, m=16, i=PACK),
+        )
+        w2_dealt = deal_words("w2_dealt", w2_raw, nc.scalar.copy, U32)
+        b_sb = [sb(f"b{i}", [P, SLOTS], F32) for i in range(PACK)]
+        x1 = sb("x1", [P, PACK, SLOTS], BF16)
+        b_ps = [psum.tile([P, 2, SLOTS], F32, name=f"b_ps{h}") for h in range(2)]
+        for i in range(PACK):
+            nc.tensor.matmul_mx(
+                out=b_ps[i // 2][:, i % 2, :], lhsT=w2_dealt[:, i * P : (i + 1) * P].bitcast(E4M3), lhsT_scale=ws_dealt[:, 0, i, :],
+                rhs=xo_codes[:].bitcast(E5M2), rhs_scale=xo_sc[:], start=True, stop=True,
+            )
+
+        for i in range(PACK):
+            nc.scalar.activation(x1[:, i, :], cq_sb[i][:].indirect(slots_cq[:]), COPY, scale=gs_sb[:, i : i + 1])
+        w_dealt = deal_words("w_dealt", w_raw, nc.scalar.copy, U32)
+        for i in range(2):
+            nc.scalar.copy(b_sb[i][:], b_ps[0][:, i, :])
+
+        spread_split_scales(vs_plane, vs_stage)
+        vs_sc = sb("vs_sc", [P, SLOTS], U8)
+        nc.vector.tensor_copy(vs_sc[:], vs_plane[:].indirect(slots_vs[:]))
+        for i in range(2):
+            nc.vector.tensor_copy(b_sb[2 + i][:], b_ps[1][:, i, :])
+
+        a_ps = [psum.tile([P, 2, SLOTS], F32, name=f"a_ps{h}") for h in range(2)]
+        a_sb = [sb(f"a{i}", [P, SLOTS], F32) for i in range(PACK)]
+        la = sb("la", [P, PACK], F32)
+
+        def first_product(h, woven):
+            codes, scales = quantize(f"x1_{h}", woven, E4M3)
+            for i in range(PACK):
+                nc.tensor.matmul_mx(
+                    out=a_ps[i // 2][:, i % 2, h * HALF : (h + 1) * HALF],
+                    lhsT=w_dealt[:, i * P : (i + 1) * P].bitcast(E5M2), lhsT_scale=ws_dealt[:, 1, i, :],
+                    rhs=codes[:].bitcast(E4M3), rhs_scale=scales[:], start=True, stop=True,
+                )
+
+        first_product(0, weave("x1_0", x1[:, :, 0:HALF]))
+        for h in range(2):
+            nc.scalar.copy(la[:, 2 * h : 2 * h + 2], a_ps[h][:, :, 0])
+        first_product(1, weave("x1_1", x1[:, :, HALF:SLOTS]))
+        vs_codes = sb("vs_codes", [P, SLOTS], U32)
+        nc.vector.tensor_copy(vs_codes[:], vs_raw[:].indirect(slots_vs[:]))
+
+        late = sb("late", [P, PACK, HALF], BF16)
+        for i in range(PACK):
+            nc.scalar.activation(late[:, i, :], b_sb[i][:].indirect(late_lists[:]), COPY, scale=la[:, i : i + 1])
+        for i in range(PACK):
+            nc.vector.tensor_copy(a_sb[i][:], a_ps[i // 2][:, i % 2, :])
+        early = sb("early", [P, PACK, HALF], BF16)
+        for i in range(PACK):
+            nc.scalar.activation(early[:, i, :], a_sb[i][:].indirect(place_lists[:]), COPY, scale=b_sb[i][:, 0:1])
+
+        def third_product(name, planes):
+            codes, scales = quantize(name, weave(name, planes), E5M2)
+            p_ps = psum.tile([P, 2, HALF], F32, name=f"{name}_ps")
+            for n in range(2):
+                nc.tensor.matmul_mx(
+                    out=p_ps[:, n, :], lhsT=vs_codes[:, n * P : (n + 1) * P].bitcast(E4M3),
+                    lhsT_scale=vs_sc[:, n * P : (n + 1) * P],
+                    rhs=codes[:].bitcast(E5M2), rhs_scale=scales[:], start=True, stop=True,
+                )
+            return p_ps
+
+        lists = {"a": cols_a, "b": cols_b}
+
+        def scatter(engine, which, n, src, d0, d1):
+            window = pages[which, n][:].indirect(lists[which][:, d0 // 16 : d1 // 16])
+            values = src[:, n, d0 % HALF : d0 % HALF + d1 - d0]
+            if engine == "vector":
+                nc.vector.tensor_copy(window, values)
+            else:
+                nc.scalar.activation(window, values, COPY)
+
+        def add_and_store(n):
+            total = sb(f"total{n}", [P, PAGE], F32)
+            nc.vector.tensor_tensor(total[:], pages["a", n][:], pages["b", n][:], ADD)
+            nc.sync.dma_start(out[n * P : (n + 1) * P, :], total[:])
+
+        late_ps = third_product("hid_late", late[:])
+        p_late = sb("p_late", [P, 2, HALF], F32)
+        nc.vector.tensor_copy(p_late[:], late_ps[:])
+        early_ps = third_product("hid_early", early[:])
+        p_early = sb("p_early", [P, 2, HALF], F32)
+        scatter("vector", "b", 0, p_late, 128, 256)
+        scatter("scalar", "a", 0, p_late, 128, 256)
+        scatter("scalar", "a", 1, p_late, 128, 256)
+        scatter("vector", "b", 1, p_late, 128, 256)
+        nc.scalar.copy(p_early[:], early_ps[:])
+        scatter("scalar", "a", 0, p_early, 0, 128)
+        scatter("vector", "b", 0, p_early, 0, 128)
+        add_and_store(0)
+        scatter("scalar", "b", 1, p_early, 0, 64)
+        scatter("scalar", "a", 1, p_early, 0, 128)
+        scatter("vector", "b", 1, p_early, 64, 128)
+        add_and_store(1)

@@ -37,6 +37,7 @@ def tile_list_groupside_codednote_store_pagetwice_kernel(
 
     with ExitStack() as ctx:
         keep = ctx.enter_context(tc.tile_pool(name="keep", bufs=1))
+        reuse = ctx.enter_context(tc.tile_pool(name="reuse", bufs=1))
         psum = ctx.enter_context(tc.psum_pool(name="psum", bufs=1))
 
         def sb(name, shape, dtype):
@@ -69,45 +70,47 @@ def tile_list_groupside_codednote_store_pagetwice_kernel(
                 start = 64 * (q // 2)
                 nc.vector.tensor_copy(plane[32 * q : 32 * q + 4, :].bitcast(I32), stage[start : start + 4, q % 2, :])
 
-        xo_raw = sb("xo_raw", [P, TABLE], U32)
-        nc.sync.dma_start(xo_raw[:].bitcast(I32), word_rows(xo_words))
-        slots_xo = load_list("slots_xo", offs2)
-        xo_stage = load_split_scales("xo_stage", xo_scales)
-        ws_stage = sb("ws_stage", [PACK, PACK, 2, HIDDEN // 4], I32)
-        nc.sync.dma_start(ws_stage[:, :, 0, :], scale_rows(w2_scales))
-        nc.sync.dma_start(ws_stage[:, :, 1, :], scale_rows(w_scales))
-        w2_raw = sb("w2_raw", [P, HIDDEN], I32)
-        nc.sync.dma_start(w2_raw[:], word_rows(w2_words))
+        def load_words(name, words, dtype):
+            raw = sb(name, [P, words.shape[2]], dtype)
+            nc.sync.dma_start(raw[:].bitcast(I32), word_rows(words))
+            return raw
+
         cq_rows = cq.rearrange("(p i) t -> i p t", i=PACK)
         cq_sb = [sb(f"cq{i}", [P, TABLE], F32) for i in range(PACK)]
         nc.sync.dma_start(cq_sb[0][:], cq_rows[0])
         slots_cq = load_list("slots_cq", offs)
         gs_sb = sb("gs_sb", [P, PACK], F32)
         nc.sync.dma_start(gs_sb[:], gs.rearrange("(p i) o -> p (i o)", i=PACK))
+        xo_stage = load_split_scales("xo_stage", xo_scales)
+        slots_xo = load_list("slots_xo", offs2)
         nc.sync.dma_start(cq_sb[1][:], cq_rows[1])
+        ws_stage = sb("ws_stage", [PACK, PACK, 2, HIDDEN // 4], I32)
+        nc.sync.dma_start(ws_stage[:, :, 0, :], scale_rows(w2_scales))
+        nc.sync.dma_start(ws_stage[:, :, 1, :], scale_rows(w_scales))
+        nc.sync.dma_start(cq_sb[2][:], cq_rows[2])
         vs_stage = load_split_scales("vs_stage", vs_scales)
         slots_vs = load_list("slots_vs", offs5)
-        for i in range(2, PACK):
-            nc.sync.dma_start(cq_sb[i][:], cq_rows[i])
-        w_raw = sb("w_raw", [P, HIDDEN], I32)
-        nc.sync.dma_start(w_raw[:], word_rows(w_words))
-        late_lists = load_list("late_lists", offs4)
-        vs_raw = sb("vs_raw", [P, TABLE], U32)
-        nc.sync.dma_start(vs_raw[:].bitcast(I32), word_rows(vs_words))
+        nc.sync.dma_start(cq_sb[3][:], cq_rows[3])
+        w_raw = load_words("w_raw", w_words, U32)
+        w2_raw = load_words("w2_raw", w2_words, U32)
+        xo_raw = reuse.tile([P, TABLE], U32, name="xo_raw", offset=0)
+        nc.sync.dma_start(xo_raw[:].bitcast(I32), word_rows(xo_words))
         place_lists = load_list("place_lists", offs3)
+        vs_raw = load_words("vs_raw", vs_words, U32)
+        late_lists = load_list("late_lists", offs4)
         cols_a = load_list("cols_a", offs6)
         cols_b = load_list("cols_b", offs7)
 
-        def deal_words(name, raw, copy, dtype):
+        def deal_words(name, raw):
             dealt = sb(name, [P, HIDDEN], U32)
-            copy(
-                dealt[:].bitcast(dtype).rearrange("p (i g m) -> p g i m", i=PACK, m=4),
-                raw[:].bitcast(dtype).rearrange("p (g m i) -> p g i m", i=PACK, m=4),
+            nc.scalar.copy(
+                dealt[:].rearrange("p (i g m) -> p g i m", i=PACK, m=4),
+                raw[:].rearrange("p (g m i) -> p g i m", i=PACK, m=4),
             )
             return dealt
 
-        def weave(name, planes):
-            woven = sb(f"{name}_woven", [P, HALF * PACK], BF16)
+        def weave(name, planes, **where):
+            woven = reuse.tile([P, HALF * PACK], BF16, name=f"{name}_woven", align_bytes=64, **where)
             nc.vector.tensor_copy(
                 woven[:].rearrange("p (g c i) -> p g i c", i=PACK, c=4),
                 planes.rearrange("p i (g c) -> p g i c", c=4),
@@ -120,8 +123,6 @@ def tile_list_groupside_codednote_store_pagetwice_kernel(
             nc.vector.quantize_mx(out=codes[:].bitcast(fmt), scales=scales[:], in_=woven[:])
             return codes, scales
 
-        xo_codes = sb("xo_codes", [P, SLOTS], U32)
-        nc.vector.tensor_copy(xo_codes[:], xo_raw[:].indirect(slots_xo[:]))
         spread_split_scales(xo_plane, xo_stage)
         xo_sc = sb("xo_sc", [P, SLOTS], U8)
         nc.vector.tensor_copy(xo_sc[:], xo_plane[:].indirect(slots_xo[:]))
@@ -134,59 +135,71 @@ def tile_list_groupside_codednote_store_pagetwice_kernel(
             ws_dealt[:].rearrange("p s i (g m) -> p s g i m", m=16),
             ws_plane[:].rearrange("p (s g m i) -> p s g i m", s=2, m=16, i=PACK),
         )
-        w2_dealt = deal_words("w2_dealt", w2_raw, nc.scalar.copy, U32)
-        b_sb = [sb(f"b{i}", [P, SLOTS], F32) for i in range(PACK)]
-        x1 = sb("x1", [P, PACK, SLOTS], BF16)
-        b_ps = [psum.tile([P, 2, SLOTS], F32, name=f"b_ps{h}") for h in range(2)]
-        for i in range(PACK):
-            nc.tensor.matmul_mx(
-                out=b_ps[i // 2][:, i % 2, :], lhsT=w2_dealt[:, i * P : (i + 1) * P].bitcast(E4M3), lhsT_scale=ws_dealt[:, 0, i, :],
-                rhs=xo_codes[:].bitcast(E5M2), rhs_scale=xo_sc[:], start=True, stop=True,
-            )
-
-        for i in range(PACK):
-            nc.scalar.activation(x1[:, i, :], cq_sb[i][:].indirect(slots_cq[:]), COPY, scale=gs_sb[:, i : i + 1])
-        w_dealt = deal_words("w_dealt", w_raw, nc.scalar.copy, U32)
-        for i in range(2):
-            nc.scalar.copy(b_sb[i][:], b_ps[0][:, i, :])
-
         spread_split_scales(vs_plane, vs_stage)
         vs_sc = sb("vs_sc", [P, SLOTS], U8)
         nc.vector.tensor_copy(vs_sc[:], vs_plane[:].indirect(slots_vs[:]))
-        for i in range(2):
-            nc.vector.tensor_copy(b_sb[2 + i][:], b_ps[1][:, i, :])
 
-        a_ps = [psum.tile([P, 2, SLOTS], F32, name=f"a_ps{h}") for h in range(2)]
-        a_sb = [sb(f"a{i}", [P, SLOTS], F32) for i in range(PACK)]
-        la = sb("la", [P, PACK], F32)
-
-        def first_product(h, woven):
-            codes, scales = quantize(f"x1_{h}", woven, E4M3)
-            for i in range(PACK):
-                nc.tensor.matmul_mx(
-                    out=a_ps[i // 2][:, i % 2, h * HALF : (h + 1) * HALF],
-                    lhsT=w_dealt[:, i * P : (i + 1) * P].bitcast(E5M2), lhsT_scale=ws_dealt[:, 1, i, :],
-                    rhs=codes[:].bitcast(E4M3), rhs_scale=scales[:], start=True, stop=True,
-                )
-
-        first_product(0, weave("x1_0", x1[:, :, 0:HALF]))
+        x1 = sb("x1", [P, PACK, SLOTS], BF16)
+        for i in range(PACK):
+            nc.scalar.activation(x1[:, i, :], cq_sb[i][:].indirect(slots_cq[:]), COPY, scale=gs_sb[:, i : i + 1])
+        w_dealt = deal_words("w_dealt", w_raw)
+        w2_dealt = deal_words("w2_dealt", w2_raw)
+        halves = [slice(0, HALF), slice(HALF, SLOTS)]
+        x1_woven = [weave(f"x1_{h}", x1[:, :, halves[h]], offset=5120 + 1024 * h) for h in range(2)]
+        x1_mx = [quantize(f"x1_{h}", x1_woven[h], E4M3) for h in range(2)]
+        xo_codes = [sb(f"xo_codes{h}", [P, HALF], U32) for h in range(2)]
         for h in range(2):
-            nc.scalar.copy(la[:, 2 * h : 2 * h + 2], a_ps[h][:, :, 0])
-        first_product(1, weave("x1_1", x1[:, :, HALF:SLOTS]))
+            nc.vector.tensor_copy(xo_codes[h][:], xo_raw[:].indirect(slots_xo[:, 8 * h : 8 * h + 8]))
         vs_codes = sb("vs_codes", [P, SLOTS], U32)
         nc.vector.tensor_copy(vs_codes[:], vs_raw[:].indirect(slots_vs[:]))
 
-        late = sb("late", [P, PACK, HALF], BF16)
-        for i in range(PACK):
-            nc.scalar.activation(late[:, i, :], b_sb[i][:].indirect(late_lists[:]), COPY, scale=la[:, i : i + 1])
-        for i in range(PACK):
-            nc.vector.tensor_copy(a_sb[i][:], a_ps[i // 2][:, i % 2, :])
+        a_ps = [psum.tile([P, SLOTS], F32, name=f"a_ps{i}") for i in range(PACK)]
+        b_ps = [psum.tile([P, 2, SLOTS], F32, name=f"b_ps{g}") for g in range(2)]
+        a_sb = [sb(f"a{i}", [P, SLOTS], F32) for i in range(2)]
+        a_sb += [reuse.tile([P, SLOTS], F32, name=f"a{2 + i}", offset=4 * SLOTS * i) for i in range(2)]
+        b_sb = [sb(f"b{i}", [P, SLOTS], F32) for i in range(PACK)]
+        lb = sb("lb", [P, PACK], F32)
         early = sb("early", [P, PACK, HALF], BF16)
-        for i in range(PACK):
-            nc.scalar.activation(early[:, i, :], a_sb[i][:].indirect(place_lists[:]), COPY, scale=b_sb[i][:, 0:1])
+        late = sb("late", [P, PACK, HALF], BF16)
 
-        def third_product(name, planes):
-            codes, scales = quantize(name, weave(name, planes), E5M2)
+        def a_product(i, h):
+            codes, scales = x1_mx[h]
+            nc.tensor.matmul_mx(
+                out=a_ps[i][:, halves[h]],
+                lhsT=w_dealt[:, i * P : (i + 1) * P].bitcast(E5M2), lhsT_scale=ws_dealt[:, 1, i, :],
+                rhs=codes[:].bitcast(E4M3), rhs_scale=scales[:], start=True, stop=True,
+            )
+
+        def b_product(i, h):
+            nc.tensor.matmul_mx(
+                out=b_ps[i // 2][:, i % 2, halves[h]],
+                lhsT=w2_dealt[:, i * P : (i + 1) * P].bitcast(E4M3), lhsT_scale=ws_dealt[:, 0, i, :],
+                rhs=xo_codes[h][:].bitcast(E5M2), rhs_scale=xo_sc[:, halves[h]], start=True, stop=True,
+            )
+
+        for g in range(2):
+            pair = (2 * g, 2 * g + 1)
+            for h in range(2):
+                for i in pair:
+                    a_product(i, h)
+            for i in pair:
+                b_product(i, 0)
+            for i in pair:
+                if g == 0:
+                    nc.scalar.copy(a_sb[i][:], a_ps[i][:])
+                else:
+                    nc.vector.tensor_copy(a_sb[i][:], a_ps[i][:])
+            nc.scalar.copy(lb[:, 2 * g : 2 * g + 2], b_ps[g][:, :, 0])
+            for i in pair:
+                nc.scalar.activation(early[:, i, :], a_sb[i][:].indirect(place_lists[:]), COPY, scale=lb[:, i : i + 1])
+        for i in range(PACK):
+            b_product(i, 1)
+
+        def copy_b(i):
+            nc.vector.tensor_copy(b_sb[i][:], b_ps[i // 2][:, i % 2, :])
+            nc.scalar.activation(late[:, i, :], b_sb[i][:].indirect(late_lists[:]), COPY, scale=a_sb[i][:, 0:1])
+
+        def third_product(name, codes, scales):
             p_ps = psum.tile([P, 2, HALF], F32, name=f"{name}_ps")
             for n in range(2):
                 nc.tensor.matmul_mx(
@@ -196,35 +209,38 @@ def tile_list_groupside_codednote_store_pagetwice_kernel(
                 )
             return p_ps
 
+        for i in range(PACK):
+            copy_b(i)
+        early_ps = third_product("early", *quantize("early", weave("early", early[:], offset=7168), E5M2))
+        p_offset = 4 * TABLE
+        late_mx = quantize("late", weave("late", late[:], offset=p_offset), E5M2)
+        late_ps = third_product("late", *late_mx)
+        p_sb = [sb("p0", [P, SLOTS], F32), reuse.tile([P, SLOTS], F32, name="p1", offset=p_offset)]
         lists = {"a": cols_a, "b": cols_b}
 
-        def scatter(engine, which, n, src, d0, d1):
+        def scatter(engine, which, n, d0, d1):
             window = pages[which, n][:].indirect(lists[which][:, d0 // 16 : d1 // 16])
-            values = src[:, n, d0 % HALF : d0 % HALF + d1 - d0]
             if engine == "vector":
-                nc.vector.tensor_copy(window, values)
+                nc.vector.tensor_copy(window, p_sb[n][:, d0:d1])
             else:
-                nc.scalar.activation(window, values, COPY)
+                nc.scalar.activation(window, p_sb[n][:, d0:d1], COPY)
 
-        def add_and_store(n):
-            total = sb(f"total{n}", [P, PAGE], F32)
-            nc.vector.tensor_tensor(total[:], pages["a", n][:], pages["b", n][:], ADD)
-            nc.sync.dma_start(out[n * P : (n + 1) * P, :], total[:])
+        def add_and_store(n, c0, c1):
+            total = sb(f"total{n}_{c0}", [P, c1 - c0], F32)
+            nc.vector.tensor_tensor(total[:], pages["a", n][:, c0:c1], pages["b", n][:, c0:c1], ADD)
+            nc.sync.dma_start(out[n * P : (n + 1) * P, c0:c1], total[:])
 
-        late_ps = third_product("hid_late", late[:])
-        p_late = sb("p_late", [P, 2, HALF], F32)
-        nc.vector.tensor_copy(p_late[:], late_ps[:])
-        early_ps = third_product("hid_early", early[:])
-        p_early = sb("p_early", [P, 2, HALF], F32)
-        scatter("vector", "b", 0, p_late, 128, 256)
-        scatter("scalar", "a", 0, p_late, 128, 256)
-        scatter("scalar", "a", 1, p_late, 128, 256)
-        scatter("vector", "b", 1, p_late, 128, 256)
-        nc.scalar.copy(p_early[:], early_ps[:])
-        scatter("scalar", "a", 0, p_early, 0, 128)
-        scatter("vector", "b", 0, p_early, 0, 128)
-        add_and_store(0)
-        scatter("scalar", "b", 1, p_early, 0, 64)
-        scatter("scalar", "a", 1, p_early, 0, 128)
-        scatter("vector", "b", 1, p_early, 64, 128)
-        add_and_store(1)
+        nc.scalar.copy(p_sb[0][:, halves[0]], early_ps[:, 0, :])
+        scatter("scalar", "a", 0, 0, HALF)
+        scatter("scalar", "b", 0, 0, HALF)
+        nc.vector.tensor_copy(p_sb[1][:, halves[0]], early_ps[:, 1, :])
+        scatter("vector", "b", 1, 0, HALF)
+        for n in range(2):
+            nc.vector.tensor_copy(p_sb[n][:, halves[1]], late_ps[:, n, :])
+        scatter("scalar", "a", 0, HALF, SLOTS)
+        scatter("vector", "b", 0, HALF, SLOTS)
+        scatter("vector", "b", 1, HALF, SLOTS)
+        scatter("scalar", "a", 1, 0, SLOTS)
+        add_and_store(0, 0, PAGE)
+        add_and_store(1, 0, PAGE // 2)
+        add_and_store(1, PAGE // 2, PAGE)

@@ -75,22 +75,22 @@ def tile_list_groupside_codednote_store_pagetwice_kernel(
             nc.sync.dma_start(raw[:].bitcast(I32), word_rows(words))
             return raw
 
-        cq_rows = cq.rearrange("(p i) t -> i p t", i=PACK)
-        cq_sb = [sb(f"cq{i}", [P, TABLE], F32) for i in range(PACK)]
-        nc.sync.dma_start(cq_sb[0][:], cq_rows[0])
-        slots_cq = load_list("slots_cq", offs)
-        gs_sb = sb("gs_sb", [P, PACK], F32)
-        nc.sync.dma_start(gs_sb[:], gs.rearrange("(p i) o -> p (i o)", i=PACK))
-        xo_stage = load_split_scales("xo_stage", xo_scales)
-        slots_xo = load_list("slots_xo", offs2)
-        nc.sync.dma_start(cq_sb[1][:], cq_rows[1])
         ws_stage = sb("ws_stage", [PACK, PACK, 2, HIDDEN // 4], I32)
         nc.sync.dma_start(ws_stage[:, :, 0, :], scale_rows(w2_scales))
         nc.sync.dma_start(ws_stage[:, :, 1, :], scale_rows(w_scales))
-        nc.sync.dma_start(cq_sb[2][:], cq_rows[2])
+        slots_cq = load_list("slots_cq", offs)
+        gs_sb = sb("gs_sb", [P, PACK], F32)
+        nc.sync.dma_start(gs_sb[:], gs.rearrange("(p i) o -> p (i o)", i=PACK))
+        cq_rows = cq.rearrange("(p i) t -> i p t", i=PACK)
+        cq_sb = [sb(f"cq{i}", [P, TABLE], F32) for i in range(PACK)]
+        nc.sync.dma_start(cq_sb[0][:], cq_rows[0])
+        xo_stage = load_split_scales("xo_stage", xo_scales)
+        nc.sync.dma_start(cq_sb[1][:], cq_rows[1])
+        slots_xo = load_list("slots_xo", offs2)
         vs_stage = load_split_scales("vs_stage", vs_scales)
         slots_vs = load_list("slots_vs", offs5)
-        nc.sync.dma_start(cq_sb[3][:], cq_rows[3])
+        for i in (2, 3):
+            nc.sync.dma_start(cq_sb[i][:], cq_rows[i])
         w_raw = load_words("w_raw", w_words, U32)
         w2_raw = load_words("w2_raw", w2_words, U32)
         xo_raw = reuse.tile([P, TABLE], U32, name="xo_raw", offset=0)
@@ -101,11 +101,11 @@ def tile_list_groupside_codednote_store_pagetwice_kernel(
         cols_a = load_list("cols_a", offs6)
         cols_b = load_list("cols_b", offs7)
 
-        def deal_words(name, raw):
+        def deal_words(name, raw, copy, dtype):
             dealt = sb(name, [P, HIDDEN], U32)
-            nc.scalar.copy(
-                dealt[:].rearrange("p (i g m) -> p g i m", i=PACK, m=4),
-                raw[:].rearrange("p (g m i) -> p g i m", i=PACK, m=4),
+            copy(
+                dealt[:].bitcast(dtype).rearrange("p (i g m) -> p g i m", i=PACK, m=4),
+                raw[:].bitcast(dtype).rearrange("p (g m i) -> p g i m", i=PACK, m=4),
             )
             return dealt
 
@@ -123,9 +123,6 @@ def tile_list_groupside_codednote_store_pagetwice_kernel(
             nc.vector.quantize_mx(out=codes[:].bitcast(fmt), scales=scales[:], in_=woven[:])
             return codes, scales
 
-        spread_split_scales(xo_plane, xo_stage)
-        xo_sc = sb("xo_sc", [P, SLOTS], U8)
-        nc.vector.tensor_copy(xo_sc[:], xo_plane[:].indirect(slots_xo[:]))
         for q in range(4):
             nc.vector.tensor_copy(
                 ws_plane[32 * q : 32 * q + 4, :].bitcast(I32), ws_stage[:, q].rearrange("p s c -> p (s c)")
@@ -135,6 +132,9 @@ def tile_list_groupside_codednote_store_pagetwice_kernel(
             ws_dealt[:].rearrange("p s i (g m) -> p s g i m", m=16),
             ws_plane[:].rearrange("p (s g m i) -> p s g i m", s=2, m=16, i=PACK),
         )
+        spread_split_scales(xo_plane, xo_stage)
+        xo_sc = sb("xo_sc", [P, SLOTS], U8)
+        nc.vector.tensor_copy(xo_sc[:], xo_plane[:].indirect(slots_xo[:]))
         spread_split_scales(vs_plane, vs_stage)
         vs_sc = sb("vs_sc", [P, SLOTS], U8)
         nc.vector.tensor_copy(vs_sc[:], vs_plane[:].indirect(slots_vs[:]))
@@ -142,8 +142,8 @@ def tile_list_groupside_codednote_store_pagetwice_kernel(
         x1 = sb("x1", [P, PACK, SLOTS], BF16)
         for i in range(PACK):
             nc.scalar.activation(x1[:, i, :], cq_sb[i][:].indirect(slots_cq[:]), COPY, scale=gs_sb[:, i : i + 1])
-        w_dealt = deal_words("w_dealt", w_raw)
-        w2_dealt = deal_words("w2_dealt", w2_raw)
+        w_dealt = deal_words("w_dealt", w_raw, nc.vector.tensor_copy, I32)
+        w2_dealt = deal_words("w2_dealt", w2_raw, nc.scalar.copy, U32)
         halves = [slice(0, HALF), slice(HALF, SLOTS)]
         x1_woven = [weave(f"x1_{h}", x1[:, :, halves[h]], offset=5120 + 1024 * h) for h in range(2)]
         x1_mx = [quantize(f"x1_{h}", x1_woven[h], E4M3) for h in range(2)]
@@ -158,7 +158,7 @@ def tile_list_groupside_codednote_store_pagetwice_kernel(
         a_sb = [sb(f"a{i}", [P, SLOTS], F32) for i in range(2)]
         a_sb += [reuse.tile([P, SLOTS], F32, name=f"a{2 + i}", offset=4 * SLOTS * i) for i in range(2)]
         b_sb = [sb(f"b{i}", [P, SLOTS], F32) for i in range(PACK)]
-        lb = sb("lb", [P, PACK], F32)
+        lb = [sb(f"lb{g}", [P, 2], F32) for g in range(2)]
         early = sb("early", [P, PACK, HALF], BF16)
         late = sb("late", [P, PACK, HALF], BF16)
 
@@ -184,14 +184,14 @@ def tile_list_groupside_codednote_store_pagetwice_kernel(
                     a_product(i, h)
             for i in pair:
                 b_product(i, 0)
-            for i in pair:
-                if g == 0:
-                    nc.scalar.copy(a_sb[i][:], a_ps[i][:])
-                else:
-                    nc.vector.tensor_copy(a_sb[i][:], a_ps[i][:])
-            nc.scalar.copy(lb[:, 2 * g : 2 * g + 2], b_ps[g][:, :, 0])
-            for i in pair:
-                nc.scalar.activation(early[:, i, :], a_sb[i][:].indirect(place_lists[:]), COPY, scale=lb[:, i : i + 1])
+            copy = nc.scalar.copy if g == 0 else nc.vector.tensor_copy
+            copy(a_sb[pair[0]][:], a_ps[pair[0]][:])
+            copy(lb[g][:], b_ps[g][:, :, 0])
+            copy(a_sb[pair[1]][:], a_ps[pair[1]][:])
+        for i in range(PACK):
+            nc.scalar.activation(
+                early[:, i, :], a_sb[i][:].indirect(place_lists[:]), COPY, scale=lb[i // 2][:, i % 2 : i % 2 + 1]
+            )
         for i in range(PACK):
             b_product(i, 1)
 

from contextlib import ExitStack

import concourse.mybir as mybir

F32 = mybir.dt.float32
BF16 = mybir.dt.bfloat16
I32 = mybir.dt.int32
U32 = mybir.dt.uint32
U16 = mybir.dt.uint16
U8 = mybir.dt.uint8
E4M3 = mybir.dt.float8_e4m3fn_x4
E5M2 = mybir.dt.float8_e5m2_x4
COPY = mybir.ActivationFunctionType.Copy
ADD = mybir.AluOpType.add

P = 128
PACK = 4
SLOTS = 256
HALF = 128
HIDDEN = 512
TABLE = 1024
PAGE = 512
FLOPS = 335544320


def tile_list_groupside_codednote_store_pagetwice_kernel(
    tc, xo_words, xo_scales, cq, gs, w_words, w_scales, w2_words, w2_scales, vs_words, vs_scales,
    offs, offs2, offs3, offs4, offs5, offs6, offs7, out,
):
    nc = tc.nc

    def word_rows(words):
        return words[0].rearrange("p c i -> p (c i)").bitcast(I32)

    def scale_rows(scales):
        return scales[0].bitcast(I32).rearrange("(q r) c -> r q c", r=PACK)

    with ExitStack() as ctx:
        keep = ctx.enter_context(tc.tile_pool(name="keep", bufs=1))
        reuse = ctx.enter_context(tc.tile_pool(name="reuse", bufs=1))
        psum = ctx.enter_context(tc.psum_pool(name="psum", bufs=1))

        def sb(name, shape, dtype):
            return keep.tile(shape, dtype, name=name, align_bytes=64)

        def load_list(name, src):
            tile = sb(name, list(src.shape), U16)
            nc.sync.dma_start(tile[:], src)
            return tile

        xo_plane = sb("xo_plane", [P, TABLE], U8)
        ws_plane = sb("ws_plane", [P, 2 * HIDDEN], U8)
        vs_plane = sb("vs_plane", [P, TABLE], U8)
        for plane in (xo_plane, ws_plane, vs_plane):
            nc.vector.memset(plane[:].bitcast(I32), 0)
        pages = {}
        for n in range(2):
            for which in "ab":
                pages[which, n] = sb(f"page_{which}{n}", [P, PAGE], F32)
                nc.vector.memset(pages[which, n][:], 0.0)

        def load_split_scales(name, scales):
            stage = sb(name, [P, 2, TABLE // 4], I32)
            for h in range(2):
                nc.sync.dma_start(stage[64 * h : 64 * h + 4], scale_rows(scales)[:, 2 * h : 2 * h + 2, :])
            return stage

        def spread_split_scales(plane, stage):
            for q in range(4):
                start = 64 * (q // 2)
                nc.vector.tensor_copy(plane[32 * q : 32 * q + 4, :].bitcast(I32), stage[start : start + 4, q % 2, :])

        def load_words(name, words, dtype):
            raw = sb(name, [P, words.shape[2]], dtype)
            nc.sync.dma_start(raw[:].bitcast(I32), word_rows(words))
            return raw

        ws_stage = sb("ws_stage", [PACK, PACK, 2, HIDDEN // 4], I32)
        nc.sync.dma_start(ws_stage[:, :, 0, :], scale_rows(w2_scales))
        nc.sync.dma_start(ws_stage[:, :, 1, :], scale_rows(w_scales))
        slots_cq = load_list("slots_cq", offs)
        gs_sb = sb("gs_sb", [P, PACK], F32)
        nc.sync.dma_start(gs_sb[:], gs.rearrange("(p i) o -> p (i o)", i=PACK))
        cq_rows = cq.rearrange("(p i) t -> i p t", i=PACK)
        cq_sb = [sb(f"cq{i}", [P, TABLE], F32) for i in range(PACK)]
        nc.sync.dma_start(cq_sb[0][:], cq_rows[0])
        xo_stage = load_split_scales("xo_stage", xo_scales)
        nc.sync.dma_start(cq_sb[1][:], cq_rows[1])
        slots_xo = load_list("slots_xo", offs2)
        vs_stage = load_split_scales("vs_stage", vs_scales)
        slots_vs = load_list("slots_vs", offs5)
        for i in (2, 3):
            nc.sync.dma_start(cq_sb[i][:], cq_rows[i])
        w_raw = load_words("w_raw", w_words, U32)
        w2_raw = load_words("w2_raw", w2_words, U32)
        xo_raw = reuse.tile([P, TABLE], U32, name="xo_raw", offset=0)
        nc.sync.dma_start(xo_raw[:].bitcast(I32), word_rows(xo_words))
        place_lists = load_list("place_lists", offs3)
        vs_raw = load_words("vs_raw", vs_words, U32)
        late_lists = load_list("late_lists", offs4)
        cols_a = load_list("cols_a", offs6)
        cols_b = load_list("cols_b", offs7)

        def deal_words(name, raw, copy, dtype):
            dealt = sb(name, [P, HIDDEN], U32)
            copy(
                dealt[:].bitcast(dtype).rearrange("p (i g m) -> p g i m", i=PACK, m=4),
                raw[:].bitcast(dtype).rearrange("p (g m i) -> p g i m", i=PACK, m=4),
            )
            return dealt

        def weave(name, planes, **where):
            woven = reuse.tile([P, HALF * PACK], BF16, name=f"{name}_woven", align_bytes=64, **where)
            nc.vector.tensor_copy(
                woven[:].rearrange("p (g c i) -> p g i c", i=PACK, c=4),
                planes.rearrange("p i (g c) -> p g i c", c=4),
            )
            return woven

        def quantize(name, woven, fmt):
            codes = sb(f"{name}_codes", [P, HALF], U32)
            scales = sb(f"{name}_scales", [P, HALF], U8)
            nc.vector.quantize_mx(out=codes[:].bitcast(fmt), scales=scales[:], in_=woven[:])
            return codes, scales

        for q in range(4):
            nc.vector.tensor_copy(
                ws_plane[32 * q : 32 * q + 4, :].bitcast(I32), ws_stage[:, q].rearrange("p s c -> p (s c)")
            )
        ws_dealt = sb("ws_dealt", [P, 2, PACK, P], U8)
        nc.vector.tensor_copy(
            ws_dealt[:].rearrange("p s i (g m) -> p s g i m", m=16),
            ws_plane[:].rearrange("p (s g m i) -> p s g i m", s=2, m=16, i=PACK),
        )
        spread_split_scales(xo_plane, xo_stage)
        xo_sc = sb("xo_sc", [P, SLOTS], U8)
        nc.vector.tensor_copy(xo_sc[:], xo_plane[:].indirect(slots_xo[:]))
        spread_split_scales(vs_plane, vs_stage)
        vs_sc = sb("vs_sc", [P, SLOTS], U8)
        nc.vector.tensor_copy(vs_sc[:], vs_plane[:].indirect(slots_vs[:]))

        x1 = sb("x1", [P, PACK, SLOTS], BF16)
        for i in range(PACK):
            nc.scalar.activation(x1[:, i, :], cq_sb[i][:].indirect(slots_cq[:]), COPY, scale=gs_sb[:, i : i + 1])
        w_dealt = deal_words("w_dealt", w_raw, nc.vector.tensor_copy, I32)
        w2_dealt = deal_words("w2_dealt", w2_raw, nc.scalar.copy, U32)
        halves = [slice(0, HALF), slice(HALF, SLOTS)]
        x1_woven = [weave(f"x1_{h}", x1[:, :, halves[h]], offset=5120 + 1024 * h) for h in range(2)]
        x1_mx = [quantize(f"x1_{h}", x1_woven[h], E4M3) for h in range(2)]
        xo_codes = [sb(f"xo_codes{h}", [P, HALF], U32) for h in range(2)]
        for h in range(2):
            nc.vector.tensor_copy(xo_codes[h][:], xo_raw[:].indirect(slots_xo[:, 8 * h : 8 * h + 8]))
        vs_codes = sb("vs_codes", [P, SLOTS], U32)
        nc.vector.tensor_copy(vs_codes[:], vs_raw[:].indirect(slots_vs[:]))

        a_ps = [psum.tile([P, SLOTS], F32, name=f"a_ps{i}") for i in range(PACK)]
        b_ps = [psum.tile([P, 2, SLOTS], F32, name=f"b_ps{g}") for g in range(2)]
        a_sb = [sb(f"a{i}", [P, SLOTS], F32) for i in range(2)]
        a_sb += [reuse.tile([P, SLOTS], F32, name=f"a{2 + i}", offset=4 * SLOTS * i) for i in range(2)]
        b_sb = [sb(f"b{i}", [P, SLOTS], F32) for i in range(PACK)]
        lb = [sb(f"lb{g}", [P, 2], F32) for g in range(2)]
        early = sb("early", [P, PACK, HALF], BF16)
        late = sb("late", [P, PACK, HALF], BF16)

        def a_product(i, h):
            codes, scales = x1_mx[h]
            nc.tensor.matmul_mx(
                out=a_ps[i][:, halves[h]],
                lhsT=w_dealt[:, i * P : (i + 1) * P].bitcast(E5M2), lhsT_scale=ws_dealt[:, 1, i, :],
                rhs=codes[:].bitcast(E4M3), rhs_scale=scales[:], start=True, stop=True,
            )

        def b_product(i, h):
            nc.tensor.matmul_mx(
                out=b_ps[i // 2][:, i % 2, halves[h]],
                lhsT=w2_dealt[:, i * P : (i + 1) * P].bitcast(E4M3), lhsT_scale=ws_dealt[:, 0, i, :],
                rhs=xo_codes[h][:].bitcast(E5M2), rhs_scale=xo_sc[:, halves[h]], start=True, stop=True,
            )

        for g in range(2):
            pair = (2 * g, 2 * g + 1)
            for h in range(2):
                for i in pair:
                    a_product(i, h)
            for i in pair:
                b_product(i, 0)
            copy = nc.scalar.copy if g == 0 else nc.vector.tensor_copy
            copy(a_sb[pair[0]][:], a_ps[pair[0]][:])
            copy(lb[g][:], b_ps[g][:, :, 0])
            copy(a_sb[pair[1]][:], a_ps[pair[1]][:])
        for i in range(PACK):
            nc.scalar.activation(
                early[:, i, :], a_sb[i][:].indirect(place_lists[:]), COPY, scale=lb[i // 2][:, i % 2 : i % 2 + 1]
            )
        for i in range(PACK):
            b_product(i, 1)

        def copy_b(i):
            nc.vector.tensor_copy(b_sb[i][:], b_ps[i // 2][:, i % 2, :])
            nc.scalar.activation(late[:, i, :], b_sb[i][:].indirect(late_lists[:]), COPY, scale=a_sb[i][:, 0:1])

        def third_product(name, codes, scales):
            p_ps = psum.tile([P, 2, HALF], F32, name=f"{name}_ps")
            for n in range(2):
                nc.tensor.matmul_mx(
                    out=p_ps[:, n, :], lhsT=vs_codes[:, n * P : (n + 1) * P].bitcast(E4M3),
                    lhsT_scale=vs_sc[:, n * P : (n + 1) * P],
                    rhs=codes[:].bitcast(E5M2), rhs_scale=scales[:], start=True, stop=True,
                )
            return p_ps

        for i in range(PACK):
            copy_b(i)
        early_ps = third_product("early", *quantize("early", weave("early", early[:], offset=7168), E5M2))
        p_offset = 4 * TABLE
        late_mx = quantize("late", weave("late", late[:], offset=p_offset), E5M2)
        late_ps = third_product("late", *late_mx)
        p_sb = [sb("p0", [P, SLOTS], F32), reuse.tile([P, SLOTS], F32, name="p1", offset=p_offset)]
        lists = {"a": cols_a, "b": cols_b}

        def scatter(engine, which, n, d0, d1):
            window = pages[which, n][:].indirect(lists[which][:, d0 // 16 : d1 // 16])
            if engine == "vector":
                nc.vector.tensor_copy(window, p_sb[n][:, d0:d1])
            else:
                nc.scalar.activation(window, p_sb[n][:, d0:d1], COPY)

        def add_and_store(n, c0, c1):
            total = sb(f"total{n}_{c0}", [P, c1 - c0], F32)
            nc.vector.tensor_tensor(total[:], pages["a", n][:, c0:c1], pages["b", n][:, c0:c1], ADD)
            nc.sync.dma_start(out[n * P : (n + 1) * P, c0:c1], total[:])

        nc.scalar.copy(p_sb[0][:, halves[0]], early_ps[:, 0, :])
        scatter("scalar", "a", 0, 0, HALF)
        scatter("scalar", "b", 0, 0, HALF)
        nc.vector.tensor_copy(p_sb[1][:, halves[0]], early_ps[:, 1, :])
        scatter("vector", "b", 1, 0, HALF)
        for n in range(2):
            nc.vector.tensor_copy(p_sb[n][:, halves[1]], late_ps[:, n, :])
        scatter("scalar", "a", 0, HALF, SLOTS)
        scatter("vector", "b", 0, HALF, SLOTS)
        scatter("vector", "b", 1, HALF, SLOTS)
        scatter("scalar", "a", 1, 0, SLOTS)
        add_and_store(0, 0, PAGE)
        add_and_store(1, 0, PAGE // 2)
        add_and_store(1, PAGE // 2, PAGE)
